import numpy as np
import ml_dtypes


def mxq(x, axis, fmt="e4m3"):
    dtype, down = {"e4m3": (ml_dtypes.float8_e4m3fn, 7), "e5m2": (ml_dtypes.float8_e5m2, 14)}[fmt]
    v = np.moveaxis(np.asarray(x, np.float32).astype(ml_dtypes.bfloat16).astype(np.float64), axis, -1)
    blocks = v.reshape(v.shape[:-1] + (-1, 32))
    amax = np.abs(blocks).max(-1, keepdims=True)
    byte = np.maximum(np.where(amax > 0, np.frexp(amax)[1] - 1 + 127, 0) - down, 1)
    scale = np.exp2(byte - 127.0)
    codes = (blocks / scale).astype(np.float32).astype(dtype).astype(np.float64)
    return np.moveaxis((codes * scale).reshape(v.shape), -1, axis)


WIDE = False


def mx_kscale(k):
    if not WIDE:
        return np.ones(k)
    levels = np.array([10, -10, 5, -5, 0])
    if k % 512:
        return np.exp2(np.random.permutation(np.resize(levels, k // 32))).repeat(32)
    a = np.empty((k // 512, 16))
    for p in range(k // 512):
        a[p, :8] = np.random.permutation(np.resize(levels, 8))
        for g in range(8):
            far = levels[np.abs(levels - a[p, g]) >= 10]
            a[p, g + 8] = far[np.random.randint(len(far))]
    return np.exp2(a.ravel()).repeat(32)


def f64(x):
    return np.asarray(x).astype(np.float64)


def striped(idx):
    return np.tile(idx.reshape(-1, 16).T, (8, 1)).astype(np.uint16)


def unstriped(offs):
    return offs[:16].T.reshape(-1).astype(np.int64)


def striped8(idx):
    return np.concatenate([x.reshape(-1, 16).T for x in idx]).astype(np.uint16)


def runs(offs, k):
    lists = np.stack([offs[16 * r : 16 * r + 16].T.reshape(-1) for r in range(8)]).astype(np.int64)
    return lists[np.arange(k) % 512 // 64]


def pack_weight(w):
    k, n = w.shape
    w = f64(np.asarray(w, np.float32).astype(ml_dtypes.bfloat16)).reshape(k // 32, 32, n)
    amax = np.abs(w).max(1)
    byte = np.clip(np.where(amax > 0, np.frexp(amax)[1] - 1 + 127 - 7, 1), 1, 254)
    scaled = (w * np.exp2(127.0 - byte)[:, None, :]).reshape(k, n).astype(np.float32)
    words = np.ascontiguousarray(scaled.reshape(k // 512, 128, 4, n).transpose(0, 1, 3, 2)).astype(ml_dtypes.float8_e4m3fn).view(np.uint8)
    return words, np.ascontiguousarray(byte.astype(np.uint8).reshape(k // 512, 16, n))


def unpack_weight(words, scales):
    g, p, n, _ = words.shape
    vals = np.ascontiguousarray(words).view(ml_dtypes.float8_e4m3fn).astype(np.float64) * np.repeat(np.exp2(scales.astype(np.float64) - 127.0), 8, axis=1)[..., None]
    return vals.transpose(0, 1, 3, 2).reshape(g * 512, n)


def relu(v):
    return np.maximum(v, 0.0)


K, T, S, N, H = 512, 2048, 512, 512, 512


def setup_inputs():
    n = np.random.standard_normal
    s = mx_kscale(K)[:, None]
    u = mx_kscale(H)
    packed_xT = pack_weight(n((K, T)) * s)
    return {
        "x_words": packed_xT[0],
        "x_scales": packed_xT[1],
        "w1": (n((K, H)) / np.sqrt(K) / s * u).astype(np.float32),
        "w2": (n((H, H)) / np.sqrt(2 * H) / u[:, None] * u).astype(np.float32),
        "w3": (n((K, H)) / np.sqrt(2 * K) / s * u).astype(np.float32),
        "res": (2 * n((N, S))).astype(np.float32),
        "w4": (n((H, N)) / np.sqrt(H) / u[:, None]).astype(np.float32),
        "offs": striped(np.random.permutation(T)[:S]),
        "nb": striped8(np.stack([np.random.permutation(S) for _ in range(8)])),
        "own": striped(np.random.permutation(T)[:S]),
        "nb2": striped8(np.stack([np.random.permutation(S) for _ in range(8)])),
    }


def reference(x_words, x_scales, w1, w2, w3, res, w4, offs, nb, own, nb2):
    xq = unpack_weight(x_words, x_scales)[:, unstriped(offs)]
    y = relu(mxq(f64(w1), 0, "e4m3").T @ xq)
    z = y[np.arange(H)[:, None], runs(nb, H)]
    x_own = unpack_weight(x_words, x_scales)[:, unstriped(own)]
    h = relu(mxq(f64(w2), 0, "e4m3").T @ mxq(z, 0, "e4m3") + mxq(f64(w3), 0, "e4m3").T @ x_own)
    z2 = h[np.arange(H)[:, None], runs(nb2, H)]
    return f64(res) + (mxq(f64(w4), 0, "e4m3").T @ mxq(z2, 0, "e4m3"))

@@ -1,0 +1,190 @@
+from contextlib import ExitStack
+
+import concourse.mybir as mybir
+
+F32 = mybir.dt.float32
+BF16 = mybir.dt.bfloat16
+I32 = mybir.dt.int32
+U32 = mybir.dt.uint32
+U16 = mybir.dt.uint16
+U8 = mybir.dt.uint8
+FP8X4 = mybir.dt.float8_e4m3fn_x4
+ACT = mybir.ActivationFunctionType
+ALU = mybir.AluOpType
+
+P = 128
+PACK = 4
+T = 2048
+S = 512
+H = 512
+LANES = 16
+FLOPS = 4 * 2 * 512 * 512 * 512
+
+
+def tile_picked_relayin_relu_p_kernel(
+    tc, x_words, x_scales, w1, w2, w3, res, w4, offs, nb, own, nb2, out
+):
+    nc = tc.nc
+    with ExitStack() as ctx:
+        keep = ctx.enter_context(tc.tile_pool(name="keep", bufs=1))
+        psum = ctx.enter_context(tc.psum_pool(name="psum", bufs=1))
+
+        def sbuf(name, shape, dtype, tag=None):
+            return keep.tile(shape, dtype, name=name, tag=tag or name, align_bytes=64)
+
+        def load_list(name, src):
+            tile = keep.tile([P, S // LANES], U16, name=name)
+            nc.sync.dma_start(tile[:], src)
+            return tile
+
+        def load_weight(name, w, c0, c1):
+            raw = sbuf(name, [P, PACK, c1 - c0], F32)
+            nc.sync.dma_start(raw[:], w.rearrange("(p j) c -> p j c", j=PACK)[:, :, c0:c1])
+            return raw
+
+        def deal(copy, dealt, raw, c0, a, b):
+            m = slice((c0 + a) // PACK, (c0 + b) // PACK)
+            copy(
+                dealt[:, :, m, :].rearrange("p t m j -> p m j t"),
+                raw[:, :, a:b].rearrange("p j (m t) -> p m j t", t=PACK),
+            )
+
+        def act_copy(dst, src):
+            nc.scalar.activation(dst, src, ACT.Copy)
+
+        def quantize(codes, scales, values):
+            nc.vector.quantize_mx(out=codes.bitcast(FP8X4), scales=scales, in_=values)
+
+        def mx_tiles(name, width, tag=None):
+            return sbuf(name + "_codes", [P, width], U32, tag), sbuf(name + "_scales", [P, width], U8)
+
+        def product(bank, weight, t, moving, cols, start, stop):
+            rows = slice(P * t, P * (t + 1))
+            nc.tensor.matmul_mx(
+                out=bank,
+                lhsT=weight[0][:, rows].bitcast(FP8X4),
+                lhsT_scale=weight[1][:, rows],
+                rhs=moving[0][:, cols].bitcast(FP8X4),
+                rhs_scale=moving[1][:, cols],
+                start=start,
+                stop=stop,
+            )
+
+        half = H // 2
+        table_scales = sbuf("table_scales", [P, T], U8)
+        nc.vector.memset(table_scales[:].bitcast(I32), 0)
+        for q in range(4):
+            nc.sync.dma_start(
+                table_scales[32 * q : 32 * q + 4, :].bitcast(I32),
+                x_scales[0, 4 * q : 4 * q + 4, :].bitcast(I32),
+            )
+        w1_raw = [load_weight("w1_raw0", w1, 0, half)]
+        offs_t = load_list("offs_t", offs)
+        own_t = load_list("own_t", own)
+        table_words = sbuf("table_words", [P, T], U32)
+        nc.sync.dma_start(
+            table_words[:].bitcast(I32), x_words[0].rearrange("p n r -> p (n r)").bitcast(I32)
+        )
+        w1_raw.append(load_weight("w1_raw1", w1, half, H))
+        nb_t = load_list("nb_t", nb)
+        w3_raw = [load_weight("w3_raw%d" % i, w3, i * half, (i + 1) * half) for i in range(2)]
+        w2_raw = [load_weight("w2_raw%d" % i, w2, i * half, (i + 1) * half) for i in range(2)]
+        nb2_t = load_list("nb2_t", nb2)
+        w4_raw = [load_weight("w4_raw%d" % i, w4, i * half, (i + 1) * half) for i in range(2)]
+        res_t = sbuf("res_t", [P, PACK, S], F32)
+        nc.sync.dma_start(res_t[:], res.rearrange("(t p) s -> p t s", t=PACK))
+
+        dealt = {n: sbuf(n + "_dealt", [P, PACK, P, PACK], BF16) for n in ("w1", "w2", "w3")}
+        wq = {n: mx_tiles(n, H) for n in ("w1", "w2", "w3")}
+
+        def quantize_weight(name, t0, t1):
+            cols = slice(P * t0, P * t1)
+            quantize(
+                wq[name][0][:, cols],
+                wq[name][1][:, cols],
+                dealt[name][:, t0:t1].rearrange("p t m j -> p (t m j)"),
+            )
+
+        picked = mx_tiles("picked", S)
+        mine_scales = sbuf("mine_scales", [P, S], U8)
+        nc.vector.tensor_copy(picked[1][:], table_scales[:].indirect(offs_t[:]))
+        nc.vector.tensor_copy(mine_scales[:], table_scales[:].indirect(own_t[:]))
+        deal(act_copy, dealt["w1"], w1_raw[0], 0, 0, half)
+        nc.vector.tensor_copy(picked[0][:], table_words[:].indirect(offs_t[:]))
+        deal(nc.scalar.copy, dealt["w1"], w1_raw[1], half, 0, 96)
+        deal(nc.vector.tensor_copy, dealt["w1"], w1_raw[1], half, 96, half)
+        for t in range(PACK):
+            quantize_weight("w1", t, t + 1)
+        mine = (sbuf("mine_codes", [P, S], U32, "w1_raw1"), mine_scales)
+        nc.vector.tensor_copy(mine[0][:], table_words[:].indirect(own_t[:]))
+
+        banks = [psum.tile([P, S], F32, name="bank%d" % b) for b in range(8)]
+        every = slice(0, S)
+
+        y = [sbuf("y%d" % t, [P, S], F32) for t in range(PACK)]
+        for t in range(PACK):
+            product(banks[t][:], wq["w1"], t, picked, every, True, True)
+            nc.scalar.activation(y[t][:], banks[t][:], ACT.Relu)
+
+        def fetch(name, planes, lists, c0, c1):
+            fetched = sbuf(name, [P, PACK, c1 - c0], BF16)
+            for t in range(PACK):
+                nc.vector.tensor_copy(
+                    fetched[:, t, :], planes[t][:].indirect(lists[:, c0 // LANES : c1 // LANES])
+                )
+            return fetched
+
+        def weave(copy, name, fetched, width, tag=None):
+            woven = sbuf(name, [P, width, PACK], BF16, tag)
+            copy(
+                woven[:].rearrange("p (c i) t -> p c t i", i=4),
+                fetched.rearrange("p t (c i) -> p c t i", i=4),
+            )
+            return woven
+
+        def quantize_woven(mx, woven, c0, c1):
+            quantize(mx[0][:, c0:c1], mx[1][:, c0:c1], woven[:].rearrange("p c t -> p (c t)"))
+
+        for i in range(2):
+            deal(nc.scalar.copy, dealt["w3"], w3_raw[i], i * half, 0, half)
+        for i in range(2):
+            deal(nc.scalar.copy, dealt["w2"], w2_raw[i], i * half, 0, half)
+
+        z = mx_tiles("z", S)
+        f0 = fetch("z_f0", y, nb_t, 0, 256)
+        v0 = weave(nc.vector.tensor_copy, "z_v0", f0[:], 256)
+        f1 = fetch("z_f1", y, nb_t, 256, 512)
+        quantize_woven(z, v0, 0, 256)
+        v1 = weave(nc.vector.tensor_copy, "z_v1", f1[:], 256)
+        quantize_weight("w3", 0, PACK)
+        quantize_woven(z, v1, 256, 512)
+        for t in range(PACK):
+            quantize_weight("w2", t, t + 1)
+
+        h = [sbuf("h%d" % t, [P, S], F32) for t in range(PACK)]
+        for t in range(PACK):
+            product(banks[PACK + t][:], wq["w3"], t, mine, every, True, False)
+        for t in range(PACK):
+            product(banks[PACK + t][:], wq["w2"], t, z, every, False, True)
+            nc.scalar.activation(h[t][:], banks[PACK + t][:], ACT.Relu)
+
+        w4q = mx_tiles("w4", H)
+        for i in range(2):
+            woven = weave(nc.scalar.copy, "w4_v%d" % i, w4_raw[i][:], half, "z_codes" if i else None)
+            quantize_woven(w4q, woven, i * half, (i + 1) * half)
+
+        out_v = out.rearrange("(t p) s -> p t s", t=PACK)
+        fetched = [fetch("z2_f%d" % i, h, nb2_t, i * 256, (i + 1) * 256) for i in range(2)]
+        width = 128
+        for i in range(4):
+            cols = slice(i * width, (i + 1) * width)
+            part = fetched[i // 2][:, :, (i % 2) * width : (i % 2 + 1) * width]
+            woven = weave(nc.scalar.copy, "z2_v%d" % i, part, width)
+            z2 = mx_tiles("z2_%d" % i, width)
+            quantize_woven(z2, woven, 0, width)
+            bank = banks[i][:].rearrange("p (t s) -> p t s", s=width)
+            for t in range(PACK):
+                product(bank[:, t, :], w4q, t, z2, slice(0, width), True, True)
+            result = sbuf("result%d" % i, [P, PACK, width], F32)
+            nc.vector.tensor_tensor(result[:], bank, res_t[:, :, cols], ALU.add)
+            nc.sync.dma_start(out_v[:, :, cols], result[:])

@@ -87,14 +87,14 @@ def tile_picked_relayin_relu_p_kernel(
         )
         w1_raw.append(load_weight("w1_raw1", w1, half, H))
         nb_t = load_list("nb_t", nb)
-        w3_raw = [load_weight("w3_raw%d" % i, w3, i * half, (i + 1) * half) for i in range(2)]
-        w2_raw = [load_weight("w2_raw%d" % i, w2, i * half, (i + 1) * half) for i in range(2)]
+        w3_raw = load_weight("w3_raw", w3, 0, H)
+        w2_raw = load_weight("w2_raw", w2, 0, H)
         nb2_t = load_list("nb2_t", nb2)
-        w4_raw = [load_weight("w4_raw%d" % i, w4, i * half, (i + 1) * half) for i in range(2)]
+        w4_raw = load_weight("w4_raw", w4, 0, H)
         res_t = sbuf("res_t", [P, PACK, S], F32)
         nc.sync.dma_start(res_t[:], res.rearrange("(t p) s -> p t s", t=PACK))
 
-        dealt = {n: sbuf(n + "_dealt", [P, PACK, P, PACK], BF16) for n in ("w1", "w2", "w3")}
+        dealt = {n: sbuf(n + "_dealt", [P, PACK, P, PACK], BF16) for n in ("w1", "w2")}
         wq = {n: mx_tiles(n, H) for n in ("w1", "w2", "w3")}
 
         def quantize_weight(name, t0, t1):
@@ -111,8 +111,8 @@ def tile_picked_relayin_relu_p_kernel(
         nc.vector.tensor_copy(mine_scales[:], table_scales[:].indirect(own_t[:]))
         deal(act_copy, dealt["w1"], w1_raw[0], 0, 0, half)
         nc.vector.tensor_copy(picked[0][:], table_words[:].indirect(offs_t[:]))
-        deal(nc.scalar.copy, dealt["w1"], w1_raw[1], half, 0, 96)
-        deal(nc.vector.tensor_copy, dealt["w1"], w1_raw[1], half, 96, half)
+        deal(nc.scalar.copy, dealt["w1"], w1_raw[1], half, 0, 128)
+        deal(nc.vector.tensor_copy, dealt["w1"], w1_raw[1], half, 128, half)
         for t in range(PACK):
             quantize_weight("w1", t, t + 1)
         mine = (sbuf("mine_codes", [P, S], U32, "w1_raw1"), mine_scales)
@@ -126,8 +126,8 @@ def tile_picked_relayin_relu_p_kernel(
             product(banks[t][:], wq["w1"], t, picked, every, True, True)
             nc.scalar.activation(y[t][:], banks[t][:], ACT.Relu)
 
-        def fetch(name, planes, lists, c0, c1):
-            fetched = sbuf(name, [P, PACK, c1 - c0], BF16)
+        def fetch(name, planes, lists, c0, c1, tag=None):
+            fetched = sbuf(name, [P, PACK, c1 - c0], BF16, tag)
             for t in range(PACK):
                 nc.vector.tensor_copy(
                     fetched[:, t, :], planes[t][:].indirect(lists[:, c0 // LANES : c1 // LANES])
@@ -145,18 +145,17 @@ def tile_picked_relayin_relu_p_kernel(
         def quantize_woven(mx, woven, c0, c1):
             quantize(mx[0][:, c0:c1], mx[1][:, c0:c1], woven[:].rearrange("p c t -> p (c t)"))
 
-        for i in range(2):
-            deal(nc.scalar.copy, dealt["w3"], w3_raw[i], i * half, 0, half)
-        for i in range(2):
-            deal(nc.scalar.copy, dealt["w2"], w2_raw[i], i * half, 0, half)
+        dealt["w3"] = sbuf("w3_dealt", [P, PACK, P, PACK], BF16, "w1_codes")
+        deal(nc.scalar.copy, dealt["w3"], w3_raw, 0, 0, H)
+        deal(nc.scalar.copy, dealt["w2"], w2_raw, 0, 0, H)
 
         z = mx_tiles("z", S)
         f0 = fetch("z_f0", y, nb_t, 0, 256)
-        v0 = weave(nc.vector.tensor_copy, "z_v0", f0[:], 256)
         f1 = fetch("z_f1", y, nb_t, 256, 512)
-        quantize_woven(z, v0, 0, 256)
-        v1 = weave(nc.vector.tensor_copy, "z_v1", f1[:], 256)
         quantize_weight("w3", 0, PACK)
+        v0 = weave(nc.vector.tensor_copy, "z_v0", f0[:], 256, "w3_raw")
+        v1 = weave(nc.vector.tensor_copy, "z_v1", f1[:], 256, "w1_codes")
+        quantize_woven(z, v0, 0, 256)
         quantize_woven(z, v1, 256, 512)
         for t in range(PACK):
             quantize_weight("w2", t, t + 1)
@@ -170,21 +169,27 @@ def tile_picked_relayin_relu_p_kernel(
 
         w4q = mx_tiles("w4", H)
         for i in range(2):
-            woven = weave(nc.scalar.copy, "w4_v%d" % i, w4_raw[i][:], half, "z_codes" if i else None)
+            woven = weave(nc.scalar.copy, "w4_v%d" % i, w4_raw[:, :, i * half : (i + 1) * half], half, "z_codes" if i else None)
             quantize_woven(w4q, woven, i * half, (i + 1) * half)
 
         out_v = out.rearrange("(t p) s -> p t s", t=PACK)
-        fetched = [fetch("z2_f%d" % i, h, nb2_t, i * 256, (i + 1) * 256) for i in range(2)]
         width = 128
+        first = fetch("z2_f0", h, nb2_t, 0, 128)
+        middle = fetch("z2_f1", h, nb2_t, 128, 384)
+        parts = [first[:], middle[:, :, 0:128], middle[:, :, 128:256]]
         for i in range(4):
             cols = slice(i * width, (i + 1) * width)
-            part = fetched[i // 2][:, :, (i % 2) * width : (i % 2 + 1) * width]
-            woven = weave(nc.scalar.copy, "z2_v%d" % i, part, width)
+            woven = weave(nc.scalar.copy, "z2_v%d" % i, parts[i], width)
             z2 = mx_tiles("z2_%d" % i, width)
             quantize_woven(z2, woven, 0, width)
+            if i == 0:
+                parts.append(fetch("z2_f2", h, nb2_t, 384, 512, "z2_f0")[:])
             bank = banks[i][:].rearrange("p (t s) -> p t s", s=width)
             for t in range(PACK):
                 product(bank[:, t, :], w4q, t, z2, slice(0, width), True, True)
-            result = sbuf("result%d" % i, [P, PACK, width], F32)
-            nc.vector.tensor_tensor(result[:], bank, res_t[:, :, cols], ALU.add)
-            nc.sync.dma_start(out_v[:, :, cols], result[:])
+            step = 2 if i == 3 else PACK
+            for t0 in range(0, PACK, step):
+                ts = slice(t0, t0 + step)
+                result = sbuf("result%d_%d" % (i, t0), [P, step, width], F32)
+                nc.vector.tensor_tensor(result[:], bank[:, ts, :], res_t[:, ts, cols], ALU.add)
+                nc.sync.dma_start(out_v[:, ts, cols], result[:])

@@ -105,6 +105,9 @@ def tile_picked_relayin_relu_p_kernel(
                 dealt[name][:, t0:t1].rearrange("p t m j -> p (t m j)"),
             )
 
+        y = [sbuf("y%d" % t, [P, 2 * S], F32) for t in range(PACK)]
+        for t in range(PACK):
+            nc.vector.memset(y[t][:, S : 2 * S], 0.0)
         picked = mx_tiles("picked", S)
         mine_scales = sbuf("mine_scales", [P, S], U8)
         nc.vector.tensor_copy(picked[1][:], table_scales[:].indirect(offs_t[:]))
@@ -113,18 +116,17 @@ def tile_picked_relayin_relu_p_kernel(
         nc.vector.tensor_copy(picked[0][:], table_words[:].indirect(offs_t[:]))
         deal(nc.scalar.copy, dealt["w1"], w1_raw[1], half, 0, 128)
         deal(nc.vector.tensor_copy, dealt["w1"], w1_raw[1], half, 128, half)
-        for t in range(PACK):
-            quantize_weight("w1", t, t + 1)
+        for t0, t1 in ((0, 1), (1, 2), (2, 4)):
+            quantize_weight("w1", t0, t1)
         mine = (sbuf("mine_codes", [P, S], U32, "w1_raw1"), mine_scales)
         nc.vector.tensor_copy(mine[0][:], table_words[:].indirect(own_t[:]))
 
         banks = [psum.tile([P, S], F32, name="bank%d" % b) for b in range(8)]
         every = slice(0, S)
 
-        y = [sbuf("y%d" % t, [P, S], F32) for t in range(PACK)]
         for t in range(PACK):
             product(banks[t][:], wq["w1"], t, picked, every, True, True)
-            nc.scalar.activation(y[t][:], banks[t][:], ACT.Relu)
+            nc.scalar.activation(y[t][:, 0:S], banks[t][:], ACT.Relu)
 
         def fetch(name, planes, lists, c0, c1, tag=None):
             fetched = sbuf(name, [P, PACK, c1 - c0], BF16, tag)
@@ -150,15 +152,14 @@ def tile_picked_relayin_relu_p_kernel(
         deal(nc.scalar.copy, dealt["w2"], w2_raw, 0, 0, H)
 
         z = mx_tiles("z", S)
-        f0 = fetch("z_f0", y, nb_t, 0, 256)
-        f1 = fetch("z_f1", y, nb_t, 256, 512)
+        f0 = fetch("z_f0", y, nb_t, 0, S)
         quantize_weight("w3", 0, PACK)
-        v0 = weave(nc.vector.tensor_copy, "z_v0", f0[:], 256, "w3_raw")
-        v1 = weave(nc.vector.tensor_copy, "z_v1", f1[:], 256, "w1_codes")
+        v0 = weave(nc.vector.tensor_copy, "z_v0", f0[:, :, 0:256], 256, "w3_raw")
+        v1 = weave(nc.vector.tensor_copy, "z_v1", f0[:, :, 256:512], 256, "w1_codes")
         quantize_woven(z, v0, 0, 256)
         quantize_woven(z, v1, 256, 512)
-        for t in range(PACK):
-            quantize_weight("w2", t, t + 1)
+        for t0, t1 in ((0, 1), (1, 2), (2, 4)):
+            quantize_weight("w2", t0, t1)
 
         h = [sbuf("h%d" % t, [P, S], F32) for t in range(PACK)]
         for t in range(PACK):
@@ -177,19 +178,29 @@ def tile_picked_relayin_relu_p_kernel(
         first = fetch("z2_f0", h, nb2_t, 0, 128)
         middle = fetch("z2_f1", h, nb2_t, 128, 384)
         parts = [first[:], middle[:, :, 0:128], middle[:, :, 128:256]]
+        z2s = []
         for i in range(4):
-            cols = slice(i * width, (i + 1) * width)
             woven = weave(nc.scalar.copy, "z2_v%d" % i, parts[i], width)
             z2 = mx_tiles("z2_%d" % i, width)
             quantize_woven(z2, woven, 0, width)
             if i == 0:
                 parts.append(fetch("z2_f2", h, nb2_t, 384, 512, "z2_f0")[:])
+            z2s.append(z2)
+        for i, tag in ((0, "z2_f1"), (1, "z2_f0")):
+            cols = slice(i * width, (i + 1) * width)
             bank = banks[i][:].rearrange("p (t s) -> p t s", s=width)
             for t in range(PACK):
-                product(bank[:, t, :], w4q, t, z2, slice(0, width), True, True)
-            step = 2 if i == 3 else PACK
-            for t0 in range(0, PACK, step):
-                ts = slice(t0, t0 + step)
-                result = sbuf("result%d_%d" % (i, t0), [P, step, width], F32)
-                nc.vector.tensor_tensor(result[:], bank[:, ts, :], res_t[:, ts, cols], ALU.add)
-                nc.sync.dma_start(out_v[:, ts, cols], result[:])
+                product(bank[:, t, :], w4q, t, z2s[i], slice(0, width), True, True)
+            result = sbuf("result%d" % i, [P, PACK, width], F32, tag)
+            nc.vector.tensor_tensor(result[:], bank, res_t[:, :, cols], ALU.add)
+            nc.sync.dma_start(out_v[:, :, cols], result[:])
+        late = [banks[2 + k][:].rearrange("p (t s) -> p t s", t=2) for k in range(2)]
+        for i in (2, 3):
+            cols = slice((i - 2) * width, (i - 1) * width)
+            for t in range(PACK):
+                product(late[t // 2][:, t % 2, cols], w4q, t, z2s[i], slice(0, width), True, True)
+        for k in range(2):
+            ts = slice(2 * k, 2 * k + 2)
+            result = sbuf("late%d" % k, [P, 2, 256], F32)
+            nc.vector.tensor_tensor(result[:], late[k], res_t[:, ts, 256:512], ALU.add)
+            nc.sync.dma_start(out_v[:, ts, 256:512], result[:])

from contextlib import ExitStack

import concourse.mybir as mybir

F32 = mybir.dt.float32
BF16 = mybir.dt.bfloat16
I32 = mybir.dt.int32
U32 = mybir.dt.uint32
U16 = mybir.dt.uint16
U8 = mybir.dt.uint8
FP8X4 = mybir.dt.float8_e4m3fn_x4
ACT = mybir.ActivationFunctionType
ALU = mybir.AluOpType

P = 128
PACK = 4
T = 2048
S = 512
H = 512
LANES = 16
FLOPS = 4 * 2 * 512 * 512 * 512


def tile_picked_relayin_relu_p_kernel(
    tc, x_words, x_scales, w1, w2, w3, res, w4, offs, nb, own, nb2, out
):
    nc = tc.nc
    with ExitStack() as ctx:
        keep = ctx.enter_context(tc.tile_pool(name="keep", bufs=1))
        psum = ctx.enter_context(tc.psum_pool(name="psum", bufs=1))

        def sbuf(name, shape, dtype, tag=None):
            return keep.tile(shape, dtype, name=name, tag=tag or name, align_bytes=64)

        def load_list(name, src):
            tile = keep.tile([P, S // LANES], U16, name=name)
            nc.sync.dma_start(tile[:], src)
            return tile

        def load_weight(name, w, c0, c1):
            raw = sbuf(name, [P, PACK, c1 - c0], F32)
            nc.sync.dma_start(raw[:], w.rearrange("(p j) c -> p j c", j=PACK)[:, :, c0:c1])
            return raw

        def deal(copy, dealt, raw, c0, a, b):
            m = slice((c0 + a) // PACK, (c0 + b) // PACK)
            copy(
                dealt[:, :, m, :].rearrange("p t m j -> p m j t"),
                raw[:, :, a:b].rearrange("p j (m t) -> p m j t", t=PACK),
            )

        def act_copy(dst, src):
            nc.scalar.activation(dst, src, ACT.Copy)

        def quantize(codes, scales, values):
            nc.vector.quantize_mx(out=codes.bitcast(FP8X4), scales=scales, in_=values)

        def mx_tiles(name, width, tag=None):
            return sbuf(name + "_codes", [P, width], U32, tag), sbuf(name + "_scales", [P, width], U8)

        def product(bank, weight, t, moving, cols, start, stop):
            rows = slice(P * t, P * (t + 1))
            nc.tensor.matmul_mx(
                out=bank,
                lhsT=weight[0][:, rows].bitcast(FP8X4),
                lhsT_scale=weight[1][:, rows],
                rhs=moving[0][:, cols].bitcast(FP8X4),
                rhs_scale=moving[1][:, cols],
                start=start,
                stop=stop,
            )

        half = H // 2
        table_scales = sbuf("table_scales", [P, T], U8)
        nc.vector.memset(table_scales[:].bitcast(I32), 0)
        for q in range(4):
            nc.sync.dma_start(
                table_scales[32 * q : 32 * q + 4, :].bitcast(I32),
                x_scales[0, 4 * q : 4 * q + 4, :].bitcast(I32),
            )
        w1_raw = [load_weight("w1_raw0", w1, 0, half)]
        offs_t = load_list("offs_t", offs)
        own_t = load_list("own_t", own)
        table_words = sbuf("table_words", [P, T], U32)
        nc.sync.dma_start(
            table_words[:].bitcast(I32), x_words[0].rearrange("p n r -> p (n r)").bitcast(I32)
        )
        w1_raw.append(load_weight("w1_raw1", w1, half, H))
        nb_t = load_list("nb_t", nb)
        w3_raw = load_weight("w3_raw", w3, 0, H)
        w2_raw = load_weight("w2_raw", w2, 0, H)
        nb2_t = load_list("nb2_t", nb2)
        w4_raw = load_weight("w4_raw", w4, 0, H)
        res_t = sbuf("res_t", [P, PACK, S], F32)
        nc.sync.dma_start(res_t[:], res.rearrange("(t p) s -> p t s", t=PACK))

        dealt = {n: sbuf(n + "_dealt", [P, PACK, P, PACK], BF16) for n in ("w1", "w2")}
        wq = {n: mx_tiles(n, H) for n in ("w1", "w2", "w3")}

        def quantize_weight(name, t0, t1):
            cols = slice(P * t0, P * t1)
            quantize(
                wq[name][0][:, cols],
                wq[name][1][:, cols],
                dealt[name][:, t0:t1].rearrange("p t m j -> p (t m j)"),
            )

        y = [sbuf("y%d" % t, [P, 2 * S], F32) for t in range(PACK)]
        for t in range(PACK):
            nc.vector.memset(y[t][:, S : 2 * S], 0.0)
        picked = mx_tiles("picked", S)
        mine_scales = sbuf("mine_scales", [P, S], U8)
        nc.vector.tensor_copy(picked[1][:], table_scales[:].indirect(offs_t[:]))
        nc.vector.tensor_copy(mine_scales[:], table_scales[:].indirect(own_t[:]))
        deal(act_copy, dealt["w1"], w1_raw[0], 0, 0, half)
        nc.vector.tensor_copy(picked[0][:], table_words[:].indirect(offs_t[:]))
        deal(nc.scalar.copy, dealt["w1"], w1_raw[1], half, 0, 128)
        deal(nc.vector.tensor_copy, dealt["w1"], w1_raw[1], half, 128, half)
        for t0, t1 in ((0, 1), (1, 2), (2, 4)):
            quantize_weight("w1", t0, t1)
        mine = (sbuf("mine_codes", [P, S], U32, "w1_raw1"), mine_scales)
        nc.vector.tensor_copy(mine[0][:], table_words[:].indirect(own_t[:]))

        banks = [psum.tile([P, S], F32, name="bank%d" % b) for b in range(8)]
        every = slice(0, S)

        for t in range(PACK):
            product(banks[t][:], wq["w1"], t, picked, every, True, True)
            nc.scalar.activation(y[t][:, 0:S], banks[t][:], ACT.Relu)

        def fetch(name, planes, lists, c0, c1, tag=None):
            fetched = sbuf(name, [P, PACK, c1 - c0], BF16, tag)
            for t in range(PACK):
                nc.vector.tensor_copy(
                    fetched[:, t, :], planes[t][:].indirect(lists[:, c0 // LANES : c1 // LANES])
                )
            return fetched

        def weave(copy, name, fetched, width, tag=None):
            woven = sbuf(name, [P, width, PACK], BF16, tag)
            copy(
                woven[:].rearrange("p (c i) t -> p c t i", i=4),
                fetched.rearrange("p t (c i) -> p c t i", i=4),
            )
            return woven

        def quantize_woven(mx, woven, c0, c1):
            quantize(mx[0][:, c0:c1], mx[1][:, c0:c1], woven[:].rearrange("p c t -> p (c t)"))

        dealt["w3"] = sbuf("w3_dealt", [P, PACK, P, PACK], BF16, "w1_codes")
        deal(nc.scalar.copy, dealt["w3"], w3_raw, 0, 0, H)
        deal(nc.scalar.copy, dealt["w2"], w2_raw, 0, 0, H)

        z = mx_tiles("z", S)
        f0 = fetch("z_f0", y, nb_t, 0, S)
        quantize_weight("w3", 0, PACK)
        v0 = weave(nc.vector.tensor_copy, "z_v0", f0[:, :, 0:256], 256, "w3_raw")
        v1 = weave(nc.vector.tensor_copy, "z_v1", f0[:, :, 256:512], 256, "w1_codes")
        quantize_woven(z, v0, 0, 256)
        quantize_woven(z, v1, 256, 512)
        for t0, t1 in ((0, 1), (1, 2), (2, 4)):
            quantize_weight("w2", t0, t1)

        h = [sbuf("h%d" % t, [P, S], F32) for t in range(PACK)]
        for t in range(PACK):
            product(banks[PACK + t][:], wq["w3"], t, mine, every, True, False)
        for t in range(PACK):
            product(banks[PACK + t][:], wq["w2"], t, z, every, False, True)
            nc.scalar.activation(h[t][:], banks[PACK + t][:], ACT.Relu)

        w4q = mx_tiles("w4", H)
        for i in range(2):
            woven = weave(nc.scalar.copy, "w4_v%d" % i, w4_raw[:, :, i * half : (i + 1) * half], half, "z_codes" if i else None)
            quantize_woven(w4q, woven, i * half, (i + 1) * half)

        out_v = out.rearrange("(t p) s -> p t s", t=PACK)
        width = 128
        first = fetch("z2_f0", h, nb2_t, 0, 128)
        middle = fetch("z2_f1", h, nb2_t, 128, 384)
        parts = [first[:], middle[:, :, 0:128], middle[:, :, 128:256]]
        z2s = []
        for i in range(4):
            woven = weave(nc.scalar.copy, "z2_v%d" % i, parts[i], width)
            z2 = mx_tiles("z2_%d" % i, width)
            quantize_woven(z2, woven, 0, width)
            if i == 0:
                parts.append(fetch("z2_f2", h, nb2_t, 384, 512, "z2_f0")[:])
            z2s.append(z2)
        for i, tag in ((0, "z2_f1"), (1, "z2_f0")):
            cols = slice(i * width, (i + 1) * width)
            bank = banks[i][:].rearrange("p (t s) -> p t s", s=width)
            for t in range(PACK):
                product(bank[:, t, :], w4q, t, z2s[i], slice(0, width), True, True)
            result = sbuf("result%d" % i, [P, PACK, width], F32, tag)
            nc.vector.tensor_tensor(result[:], bank, res_t[:, :, cols], ALU.add)
            nc.sync.dma_start(out_v[:, :, cols], result[:])
        late = [banks[2 + k][:].rearrange("p (t s) -> p t s", t=2) for k in range(2)]
        for i in (2, 3):
            cols = slice((i - 2) * width, (i - 1) * width)
            for t in range(PACK):
                product(late[t // 2][:, t % 2, cols], w4q, t, z2s[i], slice(0, width), True, True)
        for k in range(2):
            ts = slice(2 * k, 2 * k + 2)
            result = sbuf("late%d" % k, [P, 2, 256], F32)
            nc.vector.tensor_tensor(result[:], late[k], res_t[:, ts, 256:512], ALU.add)
            nc.sync.dma_start(out_v[:, ts, 256:512], result[:])
